import numpy as np
import ml_dtypes


def mxq(x, axis, fmt="e4m3"):
    dtype, down = {"e4m3": (ml_dtypes.float8_e4m3fn, 7), "e5m2": (ml_dtypes.float8_e5m2, 14)}[fmt]
    v = np.moveaxis(np.asarray(x, np.float32).astype(ml_dtypes.bfloat16).astype(np.float64), axis, -1)
    blocks = v.reshape(v.shape[:-1] + (-1, 32))
    amax = np.abs(blocks).max(-1, keepdims=True)
    byte = np.maximum(np.where(amax > 0, np.frexp(amax)[1] - 1 + 127, 0) - down, 1)
    scale = np.exp2(byte - 127.0)
    codes = (blocks / scale).astype(np.float32).astype(dtype).astype(np.float64)
    return np.moveaxis((codes * scale).reshape(v.shape), -1, axis)


WIDE = False


def mx_kscale(k):
    if not WIDE:
        return np.ones(k)
    levels = np.array([10, -10, 5, -5, 0])
    if k % 512:
        return np.exp2(np.random.permutation(np.resize(levels, k // 32))).repeat(32)
    a = np.empty((k // 512, 16))
    for p in range(k // 512):
        a[p, :8] = np.random.permutation(np.resize(levels, 8))
        for g in range(8):
            far = levels[np.abs(levels - a[p, g]) >= 10]
            a[p, g + 8] = far[np.random.randint(len(far))]
    return np.exp2(a.ravel()).repeat(32)


def f64(x):
    return np.asarray(x).astype(np.float64)


def striped(idx):
    return np.tile(idx.reshape(-1, 16).T, (8, 1)).astype(np.uint16)


def unstriped(offs):
    return offs[:16].T.reshape(-1).astype(np.int64)


def striped8(idx):
    return np.concatenate([x.reshape(-1, 16).T for x in idx]).astype(np.uint16)


def runs(offs, k):
    lists = np.stack([offs[16 * r : 16 * r + 16].T.reshape(-1) for r in range(8)]).astype(np.int64)
    return lists[np.arange(k) % 512 // 64]


def pack_weight(w):
    k, n = w.shape
    w = f64(np.asarray(w, np.float32).astype(ml_dtypes.bfloat16)).reshape(k // 32, 32, n)
    amax = np.abs(w).max(1)
    byte = np.clip(np.where(amax > 0, np.frexp(amax)[1] - 1 + 127 - 7, 1), 1, 254)
    scaled = (w * np.exp2(127.0 - byte)[:, None, :]).reshape(k, n).astype(np.float32)
    words = np.ascontiguousarray(scaled.reshape(k // 512, 128, 4, n).transpose(0, 1, 3, 2)).astype(ml_dtypes.float8_e4m3fn).view(np.uint8)
    return words, np.ascontiguousarray(byte.astype(np.uint8).reshape(k // 512, 16, n))


def unpack_weight(words, scales):
    g, p, n, _ = words.shape
    vals = np.ascontiguousarray(words).view(ml_dtypes.float8_e4m3fn).astype(np.float64) * np.repeat(np.exp2(scales.astype(np.float64) - 127.0), 8, axis=1)[..., None]
    return vals.transpose(0, 1, 3, 2).reshape(g * 512, n)


def sigmoid(v):
    return 1.0 / (1.0 + np.exp(-np.maximum(v, -700.0)))


K, T, S, H, W = 512, 2048, 512, 512, 2048


def setup_inputs():
    n = np.random.standard_normal
    s = mx_kscale(K)[:, None]
    u = mx_kscale(S)
    packed_xT = pack_weight(n((K, T)) * s)
    return {
        "x_words": packed_xT[0],
        "x_scales": packed_xT[1],
        "w1": (n((K, H)) / np.sqrt(K) / s).astype(np.float32),
        "sl": np.random.uniform(1.5, 3.0, (H, 1)).astype(np.float32),
        "th": (0.5 * n((H, 1))).astype(np.float32),
        "sl2": np.random.uniform(1.0, 2.0, (H, 1)).astype(np.float32),
        "th2": (0.5 * n((H, 1))).astype(np.float32),
        "ga": (np.random.uniform(0.5, 1.5, (H, 1)) * u[:, None]).astype(np.float32),
        "gb": (np.random.uniform(0.5, 1.5, (H, 1)) / u[:, None]).astype(np.float32),
        "tau": np.random.uniform(0.3, 0.9, (S, 1)).astype(np.float32),
        "offs": striped(np.random.permutation(T)[:S]),
        "n1": striped(np.random.randint(0, S, W)),
        "n2": striped8(np.stack([np.random.permutation(S) for _ in range(8)])),
        "n3": striped8(np.stack([np.random.permutation(S) for _ in range(8)])),
        "n4": striped(np.random.permutation(S)),
        "n5": striped(np.random.permutation(S)),
    }


def reference(x_words, x_scales, w1, sl, th, sl2, th2, ga, gb, tau, offs, n1, n2, n3, n4, n5):
    xq = unpack_weight(x_words, x_scales)[:, unstriped(offs)]
    y = mxq(f64(w1), 0, "e4m3").T @ xq
    sg = sigmoid(f64(sl) * (y[:, unstriped(n1)] - f64(th)))
    cnt = sg.reshape(H, S, 4).sum(axis=2)
    z = f64(ga) * np.maximum(y, cnt + -1.5)
    sg2 = sigmoid(f64(sl2) * (y[np.arange(H)[:, None], runs(n2, H)] - f64(th2)))
    z2 = f64(gb) * (np.maximum(y * sg2, 0.75 * (y[np.arange(H)[:, None], runs(n3, H)])))
    s = 0.0625 * ((mxq(z, 0, "e4m3").T @ mxq(z2, 0, "e4m3")))
    low = s.min(axis=1, keepdims=True)
    ea = np.exp(f64(tau) * (low - s[:, unstriped(n4)]))
    return s - (2.0 * (ea * s[:, unstriped(n5)]))

@@ -1,0 +1,408 @@
+from contextlib import ExitStack
+
+import concourse.mybir as mybir
+from concourse.masks import make_identity
+
+FLOPS = 2 * 2 * 512 * 512 * 512
+
+F32 = mybir.dt.float32
+BF16 = mybir.dt.bfloat16
+I32 = mybir.dt.int32
+U32 = mybir.dt.uint32
+U16 = mybir.dt.uint16
+U8 = mybir.dt.uint8
+FP8X4 = mybir.dt.float8_e4m3fn_x4
+ALU = mybir.AluOpType
+ACT = mybir.ActivationFunctionType
+
+P = 128
+PACK = 4
+T = 2048
+S = 512
+MEMBERS = 4
+BLOCKS = S // P
+WINDOW = 2 * S
+LIST_COLS = S // 16
+
+
+def tile_picked_selfegcemoebz_none_p_kernel(
+    tc, x_words, x_scales, w1, sl, th, sl2, th2, ga, gb, tau, offs, n1, n2, n3, n4, n5, out
+):
+    nc = tc.nc
+    with ExitStack() as ctx:
+        keep = ctx.enter_context(tc.tile_pool(name="keep", bufs=1))
+        psum = ctx.enter_context(tc.psum_pool(name="psum", bufs=1))
+
+        def load_list(name, src):
+            tile = keep.tile(list(src.shape), U16, name=name)
+            nc.sync.dma_start(tile[:], src)
+            return tile
+
+        def load_by_feature(name, src, queue):
+            tile = keep.tile([P, PACK], F32, name=name)
+            queue.dma_start(out=tile[:], in_=src.rearrange("(p t) o -> p (t o)", t=PACK))
+            return tile
+
+        scale_table = keep.tile([P, T], U8, name="scale_table")
+        nc.gpsimd.memset(scale_table[:].bitcast(I32), 0)
+        w_rows = w1.rearrange("(p j) c -> p j c", j=PACK)
+        w_raw = [keep.tile([P, PACK, S // 2], F32, name="w_raw%d" % h) for h in range(2)]
+        nc.sync.dma_start(out=w_raw[0][:], in_=w_rows[:, :, : S // 2])
+        offs_sb = load_list("offs_sb", offs)
+        for q in range(4):
+            nc.sync.dma_start(
+                out=scale_table[32 * q : 32 * q + 4, :].bitcast(I32),
+                in_=x_scales[0, 4 * q : 4 * q + 4, :].bitcast(I32),
+            )
+        nc.sync.dma_start(out=w_raw[1][:], in_=w_rows[:, :, S // 2 :])
+        word_table = keep.tile([P, T], U32, name="word_table")
+        nc.sync.dma_start(
+            out=word_table[:].bitcast(I32),
+            in_=x_words[0].rearrange("p n r -> p (n r)").bitcast(I32),
+        )
+
+        def sigmoid_bias(name, slope, threshold):
+            product = keep.tile([P, PACK], F32, name=name + "_product")
+            nc.gpsimd.tensor_tensor(product[:], slope[:], threshold[:], ALU.mult)
+            bias = keep.tile([P, PACK], F32, name=name)
+            nc.gpsimd.tensor_scalar(bias[:], product[:], -1.0, 0.0, ALU.mult, ALU.add)
+            return bias
+
+        n2_sb = load_list("n2_sb", n2)
+        sl2_sb = load_by_feature("sl2_sb", sl2, nc.gpsimd)
+        th2_sb = load_by_feature("th2_sb", th2, nc.gpsimd)
+        n3_sb = load_list("n3_sb", n3)
+        n1_sb = load_list("n1_sb", n1)
+        sl_sb = load_by_feature("sl_sb", sl, nc.sync)
+        th_sb = load_by_feature("th_sb", th, nc.sync)
+        gb_sb = load_by_feature("gb_sb", gb, nc.sync)
+        ga_sb = load_by_feature("ga_sb", ga, nc.sync)
+        tau_sb = keep.tile([P, BLOCKS], F32, name="tau_sb")
+        with nc.allow_non_contiguous_dma(reason="one value of tau a partition and block"):
+            nc.sync.dma_start(out=tau_sb[:], in_=tau.rearrange("(b p) o -> p (b o)", p=P))
+        n4_sb = load_list("n4_sb", n4)
+        n5_sb = load_list("n5_sb", n5)
+        bias2 = sigmoid_bias("bias2", sl2_sb, th2_sb)
+        ident = keep.tile([P, P], F32, name="ident")
+        make_identity(nc, ident[:])
+        bias1 = sigmoid_bias("bias1", sl_sb, th_sb)
+        neg_tau = keep.tile([P, BLOCKS], F32, name="neg_tau")
+        nc.gpsimd.tensor_scalar(neg_tau[:], tau_sb[:], -1.0, 0.0, ALU.mult, ALU.add)
+
+        y_win = [keep.tile([P, WINDOW], F32, name="y_win%d" % t) for t in range(PACK)]
+        s_win = [keep.tile([P, WINDOW], F32, name="s_win%d" % b) for b in range(BLOCKS)]
+        for win in y_win:
+            nc.vector.memset(win[:, S:], 0.0)
+
+        w_grouped = keep.tile([P, PACK, P, PACK], BF16, name="w_grouped", align_bytes=64)
+        for h in range(2):
+            nc.vector.tensor_copy(
+                out=w_grouped[:, :, h * (P // 2) : (h + 1) * (P // 2), :].rearrange("p t m j -> p m j t"),
+                in_=w_raw[h][:].rearrange("p j (m t) -> p m j t", t=PACK),
+            )
+        x_scale = keep.tile([P, S], U8, name="x_scale", align_bytes=64)
+        nc.vector.tensor_copy(x_scale[:], scale_table[:].indirect(offs_sb[:]))
+        w_codes = keep.tile([P, S], U32, name="w_codes", align_bytes=64)
+        w_scale = keep.tile([P, S], U8, name="w_scale", align_bytes=64)
+        nc.vector.quantize_mx(
+            out=w_codes[:].bitcast(FP8X4),
+            scales=w_scale[:],
+            in_=w_grouped[:].rearrange("p t m j -> p (t m j)"),
+        )
+        x_codes = keep.tile([P, S], U32, name="x_codes", align_bytes=64)
+        nc.vector.tensor_copy(x_codes[:], word_table[:].indirect(offs_sb[:]))
+
+        for t in range(PACK):
+            cols = slice(t * P, (t + 1) * P)
+            acc = psum.tile([P, S], F32, name="y_acc%d" % t, tag="product", bufs=4)
+            nc.tensor.matmul_mx(
+                out=acc[:],
+                lhsT=w_codes[:, cols].bitcast(FP8X4),
+                lhsT_scale=w_scale[:, cols],
+                rhs=x_codes[:].bitcast(FP8X4),
+                rhs_scale=x_scale[:],
+                start=True,
+                stop=True,
+            )
+            nc.vector.tensor_copy(y_win[t][:, :S], acc[:])
+
+        sg2, sg, y3, gated, larger2, y_turned, larger, z_grouped, s_acc, exp_bias = ({} for k in range(10))
+
+        def gate2(t):
+            sg2[t] = keep.tile([P, S], F32, name="sg2_%d" % t, tag="sg2_%d" % t, align_bytes=64)
+            nc.scalar.activation(
+                sg2[t][:], y_win[t][:].indirect(n2_sb[:]), ACT.Sigmoid,
+                bias=bias2[:, t : t + 1], scale=sl2_sb[:, t : t + 1],
+            )
+
+        held = {}
+        pins = {"larger0": "larger2_2", "larger1": "z2_grouped", "larger2": "z_grouped1", "larger3": "z_grouped2"}
+        reused = {}
+
+        def members(b, t):
+            chunk = b * PACK + t
+            if chunk not in held:
+                name = "sg_%d" % chunk
+                tag, n = reused.get(chunk, (name, 1))
+                tile = keep.tile([P, n * S], F32, name=name, tag=tag, align_bytes=64)
+                for k in range(n):
+                    held[chunk + k] = tile[:, k * S : (k + 1) * S]
+            sg[b, t] = held[chunk]
+            nc.scalar.activation(
+                sg[b, t],
+                y_win[t][:].indirect(n1_sb[:, b * LIST_COLS : (b + 1) * LIST_COLS]),
+                ACT.Sigmoid,
+                bias=bias1[:, t : t + 1], scale=sl_sb[:, t : t + 1],
+            )
+
+        def fetch3(t):
+            y3[t] = keep.tile([P, S], F32, name="y3_%d" % t, tag="y3_%d" % t, align_bytes=64)
+            nc.vector.tensor_copy(y3[t][:], y_win[t][:].indirect(n3_sb[:]))
+
+        def apply_gate(t):
+            gated[t] = s_win[t][:, S:]
+            nc.vector.tensor_tensor(gated[t], y_win[t][:, :S], sg2[t][:], ALU.mult)
+
+        def compare2(t):
+            larger2[t] = keep.tile([P, S], F32, name="larger2_%d" % t, tag="larger2_%d" % t, align_bytes=64)
+            nc.vector.scalar_tensor_tensor(larger2[t][:], y3[t][:], 0.75, gated[t], ALU.mult, ALU.max)
+
+        z2_rows = keep.tile([P, PACK, S], BF16, name="z2_rows", tag="z2_rows", align_bytes=64)
+
+        def weigh2(t):
+            nc.vector.tensor_scalar(z2_rows[:, t, :], larger2[t][:], gb_sb[:, t : t + 1], None, ALU.mult)
+
+        z2_grouped = keep.tile([P, S, PACK], BF16, name="z2_grouped", tag="z2_grouped", align_bytes=64)
+        z2_codes = keep.tile([P, S], U32, name="z2_codes", align_bytes=64)
+        z2_scale = keep.tile([P, S], U8, name="z2_scale", align_bytes=64)
+
+        def group2():
+            nc.vector.tensor_copy(
+                out=z2_grouped[:].rearrange("p (c i) t -> p c t i", i=4),
+                in_=z2_rows[:].rearrange("p t (c i) -> p c t i", i=4),
+            )
+
+        def quantise2():
+            nc.vector.quantize_mx(
+                out=z2_codes[:].bitcast(FP8X4), scales=z2_scale[:],
+                in_=z2_grouped[:].rearrange("p c t -> p (c t)"),
+            )
+
+        def turn_y(b):
+            turn = psum.tile([P, PACK, P], F32, name="y_turn%d" % b, tag="product", bufs=4)
+            for t in range(PACK):
+                nc.tensor.transpose(turn[:, t, :], y_win[t][:, b * P : (b + 1) * P], ident[:])
+            y_turned[b] = keep.tile([P, S], F32, name="y_turned%d" % b, tag="y_turned%d" % b, align_bytes=64)
+            nc.vector.tensor_copy(y_turned[b][:], turn[:].rearrange("j t p -> j (t p)"))
+
+        cnt = {}
+        pairs = {}
+        paired = {9: ("z2_rows", 3, nc.gpsimd), 12: ("z_grouped0", 2, nc.gpsimd), 14: ("y_turned2", 2, nc.gpsimd)}
+
+        def count(b, t):
+            if t == 0:
+                if b == 2:
+                    cnt[b] = psum.tile([P, PACK, P], F32, name="cnt%d" % b, tag="product", bufs=4)
+                else:
+                    cnt[b] = psum.tile([P, PACK, P], F32, name="cnt%d" % b, tag="cnt", bufs=2)
+            terms = sg[b, t].rearrange("p (j u) -> p j u", u=MEMBERS)
+            chunk = b * PACK + t
+            if chunk in paired:
+                tag, n, engine = paired[chunk]
+                tile = keep.tile([P, n * 2 * P], F32, name="pairs%d" % chunk, tag=tag or "pairs%d" % chunk, align_bytes=64)
+                for k in range(n):
+                    pairs[chunk + k] = (tile[:, k * 2 * P : (k + 1) * 2 * P].rearrange("p (j u) -> p j u", u=2), engine)
+            if chunk in pairs:
+                halves, engine = pairs[chunk]
+                engine.tensor_tensor(halves, terms[:, :, 0:2], terms[:, :, 2:4], ALU.add)
+                terms = halves
+            n = terms.shape[2]
+            for u in range(n):
+                nc.tensor.matmul(
+                    cnt[b][:, t, :], terms[:, :, u], ident[:],
+                    start=(u == 0), stop=(u == n - 1), is_transpose=True,
+                )
+
+        def compare(b):
+            larger[b] = keep.tile([P, PACK, P], F32, name="larger%d" % b, tag=pins.get("larger%d" % b, "larger%d" % b), align_bytes=64)
+            nc.vector.scalar_tensor_tensor(
+                larger[b][:].rearrange("j t p -> j (t p)"), cnt[b][:].rearrange("j t p -> j (t p)"), -1.5,
+                y_turned[b][:], ALU.add, ALU.max,
+            )
+
+        back = {}
+
+        def turn_back(b):
+            back[b] = psum.tile([P, PACK, P], F32, name="back%d" % b, tag="turn", bufs=2)
+            for t in range(PACK):
+                nc.tensor.transpose(back[b][:, t, :], larger[b][:, t, :], ident[:])
+
+        def weigh(b):
+            z_grouped[b] = keep.tile([P, P, PACK], BF16, name="z_grouped%d" % b, tag="z_grouped%d" % b, align_bytes=64)
+            nc.vector.tensor_tensor(
+                z_grouped[b][:], back[b][:].rearrange("p t j -> p j t"),
+                ga_sb[:].unsqueeze(1).to_broadcast([P, P, PACK]), ALU.mult,
+            )
+
+        z_codes, z_scale = {}, {}
+
+        def quantise(b):
+            z_codes[b] = keep.tile([P, P], U32, name="z_codes%d" % b, tag="z_codes%d" % b, align_bytes=64)
+            z_scale[b] = keep.tile([P, P], U8, name="z_scale%d" % b, align_bytes=64)
+            nc.vector.quantize_mx(
+                out=z_codes[b][:].bitcast(FP8X4), scales=z_scale[b][:],
+                in_=z_grouped[b][:].rearrange("p j t -> p (j t)"),
+            )
+
+        def second_product(b):
+            acc = psum.tile([P, S], F32, name="s_acc%d" % b, tag="product", bufs=4)
+            nc.tensor.matmul_mx(
+                out=acc[:],
+                lhsT=z_codes[b][:].bitcast(FP8X4),
+                lhsT_scale=z_scale[b][:],
+                rhs=z2_codes[:].bitcast(FP8X4),
+                rhs_scale=z2_scale[:],
+                start=True,
+                stop=True,
+            )
+            s_acc[b] = acc
+
+        def leave_bank(b):
+            acc = s_acc[b]
+            low = keep.tile([P, 1], F32, name="low%d" % b)
+            nc.vector.tensor_scalar(s_win[b][:, :S], acc[:], 0.0625, None, ALU.mult, ALU.min, accum_out=low[:])
+            exp_bias[b] = keep.tile([P, 1], F32, name="exp_bias%d" % b)
+            nc.gpsimd.tensor_tensor(exp_bias[b][:], low[:], tau_sb[:, b : b + 1], ALU.mult)
+
+        fetched = {}
+
+        def fetch5(b, engine):
+            fetched[b] = keep.tile([P, S], F32, name="s5_%d" % b, tag=pins.get("s5_%d" % b, "s5_%d" % b), align_bytes=64)
+            if engine == "scalar":
+                nc.scalar.activation(fetched[b][:], s_win[b][:].indirect(n5_sb[:]), ACT.Copy)
+            else:
+                nc.vector.tensor_copy(fetched[b][:], s_win[b][:].indirect(n5_sb[:]))
+
+        def block_members(b, ts):
+            for t in ts:
+                members(b, t)
+                count(b, t)
+
+        gate2(0)
+        gate2(1)
+        gate2(2)
+        gate2(3)
+        turn_y(0)
+        turn_y(1)
+        turn_y(2)
+        turn_y(3)
+        members(0, 0)
+        members(0, 1)
+        members(0, 2)
+        members(0, 3)
+        members(1, 0)
+        members(1, 1)
+        members(1, 2)
+        members(1, 3)
+        members(2, 0)
+        members(2, 1)
+        members(2, 2)
+        members(2, 3)
+        members(3, 0)
+        members(3, 1)
+        members(3, 2)
+        members(3, 3)
+        count(0, 0)
+        count(0, 1)
+        count(0, 2)
+        count(0, 3)
+        count(1, 0)
+        count(1, 1)
+        count(1, 2)
+        count(1, 3)
+        count(2, 0)
+        fetch3(0)
+        apply_gate(0)
+        fetch3(1)
+        compare2(0)
+        apply_gate(1)
+        weigh2(0)
+        fetch3(2)
+        compare2(1)
+        apply_gate(2)
+        weigh2(1)
+        fetch3(3)
+        compare2(2)
+        apply_gate(3)
+        weigh2(2)
+        compare2(3)
+        compare(0)
+        turn_back(0)
+        weigh2(3)
+        group2()
+        count(2, 1)
+        count(2, 2)
+        count(2, 3)
+        quantise2()
+        compare(1)
+        turn_back(1)
+        weigh(0)
+        weigh(1)
+        quantise(0)
+        second_product(0)
+        count(3, 0)
+        count(3, 1)
+        quantise(1)
+        second_product(1)
+        leave_bank(0)
+        compare(2)
+        turn_back(2)
+        count(3, 2)
+        count(3, 3)
+        leave_bank(1)
+        fetch5(0, "vector")
+        weigh(2)
+        quantise(2)
+        second_product(2)
+        compare(3)
+        turn_back(3)
+        leave_bank(2)
+        weigh(3)
+        quantise(3)
+        second_product(3)
+
+        ea = keep.tile([P, BLOCKS, S], F32, name="ea")
+
+        def decay(b):
+            nc.scalar.activation(
+                ea[:, b, :], s_win[b][:].indirect(n4_sb[:]), ACT.Exp,
+                bias=exp_bias[b][:], scale=neg_tau[:, b : b + 1],
+            )
+
+
+        weighted = keep.tile([P, BLOCKS, S], F32, name="weighted", tag="z_grouped%d" % (BLOCKS - 1), align_bytes=64)
+
+        def weight5(b):
+            s5 = fetched[b][:] if b in fetched else s_win[b][:].indirect(n5_sb[:])
+            nc.vector.tensor_tensor(weighted[:, b, :], s5, ea[:, b, :], ALU.mult)
+
+        def finish(b):
+            result = keep.tile([P, S], F32, name="result%d" % b)
+            nc.vector.scalar_tensor_tensor(result[:], weighted[:, b, :], -2.0, s_win[b][:, :S], ALU.mult, ALU.add)
+            nc.sync.dma_start(out=out[b * P : (b + 1) * P, :], in_=result[:])
+
+        decay(0)
+        decay(1)
+        decay(2)
+        fetch5(2, "scalar")
+        weight5(0)
+        leave_bank(3)
+        decay(3)
+        fetch5(3, "scalar")
+        finish(0)
+        weight5(1)
+        weight5(2)
+        finish(1)
+        finish(2)
+        weight5(3)
+        finish(3)

@@ -23,6 +23,7 @@ MEMBERS = 4
 BLOCKS = S // P
 WINDOW = 2 * S
 LIST_COLS = S // 16
+HALF = S // 2
 
 
 def tile_picked_selfegcemoebz_none_p_kernel(
@@ -42,6 +43,11 @@ def tile_picked_selfegcemoebz_none_p_kernel(
             tile = keep.tile([P, PACK], F32, name=name)
             queue.dma_start(out=tile[:], in_=src.rearrange("(p t) o -> p (t o)", t=PACK))
             return tile
+
+        warm_in = keep.tile([P, 1], F32, name="warm_in")
+        warm_out = keep.tile([P, 1], F32, name="warm_out")
+        nc.vector.memset(warm_in[:], 0.0)
+        nc.scalar.activation(warm_out[:], warm_in[:], ACT.Sigmoid)
 
         scale_table = keep.tile([P, T], U8, name="scale_table")
         nc.gpsimd.memset(scale_table[:].bitcast(I32), 0)
@@ -95,10 +101,10 @@ def tile_picked_selfegcemoebz_none_p_kernel(
             nc.vector.memset(win[:, S:], 0.0)
 
         w_grouped = keep.tile([P, PACK, P, PACK], BF16, name="w_grouped", align_bytes=64)
-        for h in range(2):
-            nc.vector.tensor_copy(
-                out=w_grouped[:, :, h * (P // 2) : (h + 1) * (P // 2), :].rearrange("p t m j -> p m j t"),
-                in_=w_raw[h][:].rearrange("p j (m t) -> p m j t", t=PACK),
+        for h, cast in enumerate((nc.scalar.copy, nc.vector.tensor_copy)):
+            cast(
+                w_grouped[:, :, h * (P // 2) : (h + 1) * (P // 2), :],
+                w_raw[h][:].rearrange("p j (m t) -> p t m j", t=PACK),
             )
         x_scale = keep.tile([P, S], U8, name="x_scale", align_bytes=64)
         nc.vector.tensor_copy(x_scale[:], scale_table[:].indirect(offs_sb[:]))
@@ -110,21 +116,30 @@ def tile_picked_selfegcemoebz_none_p_kernel(
             in_=w_grouped[:].rearrange("p t m j -> p (t m j)"),
         )
         x_codes = keep.tile([P, S], U32, name="x_codes", align_bytes=64)
-        nc.vector.tensor_copy(x_codes[:], word_table[:].indirect(offs_sb[:]))
+        for h in range(2):
+            nc.vector.tensor_copy(
+                x_codes[:, h * HALF : (h + 1) * HALF],
+                word_table[:].indirect(offs_sb[:, h * LIST_COLS // 2 : (h + 1) * LIST_COLS // 2]),
+            )
 
-        for t in range(PACK):
-            cols = slice(t * P, (t + 1) * P)
-            acc = psum.tile([P, S], F32, name="y_acc%d" % t, tag="product", bufs=4)
+        def first_product(t, cols, leave, tag, bufs):
+            feats = slice(t * P, (t + 1) * P)
+            acc = psum.tile([P, cols.stop - cols.start], F32, name="y_acc%d_%d" % (t, cols.start), tag=tag, bufs=bufs)
             nc.tensor.matmul_mx(
                 out=acc[:],
-                lhsT=w_codes[:, cols].bitcast(FP8X4),
-                lhsT_scale=w_scale[:, cols],
-                rhs=x_codes[:].bitcast(FP8X4),
-                rhs_scale=x_scale[:],
+                lhsT=w_codes[:, feats].bitcast(FP8X4),
+                lhsT_scale=w_scale[:, feats],
+                rhs=x_codes[:, cols].bitcast(FP8X4),
+                rhs_scale=x_scale[:, cols],
                 start=True,
                 stop=True,
             )
-            nc.vector.tensor_copy(y_win[t][:, :S], acc[:])
+            leave(y_win[t][:, cols], acc[:])
+
+        first_product(0, slice(0, HALF), nc.scalar.copy, "turn", 1)
+        first_product(0, slice(HALF, S), nc.scalar.copy, "product", 4)
+        for t in range(1, PACK):
+            first_product(t, slice(0, S), nc.vector.tensor_copy, "product", 4)
 
         sg2, sg, y3, gated, larger2, y_turned, larger, z_grouped, s_acc, exp_bias = ({} for k in range(10))
 
@@ -136,7 +151,7 @@ def tile_picked_selfegcemoebz_none_p_kernel(
             )
 
         held = {}
-        pins = {"larger0": "larger2_2", "larger1": "z2_grouped", "larger2": "z_grouped1", "larger3": "z_grouped2"}
+        pins = {"larger0": "sg2_3", "larger1": "z2_grouped", "z_grouped0": "z2_rows", "last_count3": "z_grouped2", "s5_0": "z_grouped1"}
         reused = {}
 
         def members(b, t):
@@ -170,7 +185,7 @@ def tile_picked_selfegcemoebz_none_p_kernel(
         z2_rows = keep.tile([P, PACK, S], BF16, name="z2_rows", tag="z2_rows", align_bytes=64)
 
         def weigh2(t):
-            nc.vector.tensor_scalar(z2_rows[:, t, :], larger2[t][:], gb_sb[:, t : t + 1], None, ALU.mult)
+            (nc.gpsimd if t in (0, 1, 2) else nc.vector).tensor_scalar(z2_rows[:, t, :], larger2[t][:], gb_sb[:, t : t + 1], 0.0, ALU.mult, ALU.add)
 
         z2_grouped = keep.tile([P, S, PACK], BF16, name="z2_grouped", tag="z2_grouped", align_bytes=64)
         z2_codes = keep.tile([P, S], U32, name="z2_codes", align_bytes=64)
@@ -197,14 +212,12 @@ def tile_picked_selfegcemoebz_none_p_kernel(
 
         cnt = {}
         pairs = {}
-        paired = {9: ("z2_rows", 3, nc.gpsimd), 12: ("z_grouped0", 2, nc.gpsimd), 14: ("y_turned2", 2, nc.gpsimd)}
+        paired = {8: ("y_turned1", 7, nc.gpsimd)}
 
         def count(b, t):
             if t == 0:
-                if b == 2:
-                    cnt[b] = psum.tile([P, PACK, P], F32, name="cnt%d" % b, tag="product", bufs=4)
-                else:
-                    cnt[b] = psum.tile([P, PACK, P], F32, name="cnt%d" % b, tag="cnt", bufs=2)
+                if True:
+                    cnt[b] = psum.tile([P, PACK, P], F32, name="cnt%d" % b, tag="cnt", bufs=3)
             terms = sg[b, t].rearrange("p (j u) -> p j u", u=MEMBERS)
             chunk = b * PACK + t
             if chunk in paired:
@@ -233,12 +246,12 @@ def tile_picked_selfegcemoebz_none_p_kernel(
         back = {}
 
         def turn_back(b):
-            back[b] = psum.tile([P, PACK, P], F32, name="back%d" % b, tag="turn", bufs=2)
+            back[b] = psum.tile([P, PACK, P], F32, name="back%d" % b, tag="turn", bufs=1)
             for t in range(PACK):
                 nc.tensor.transpose(back[b][:, t, :], larger[b][:, t, :], ident[:])
 
         def weigh(b):
-            z_grouped[b] = keep.tile([P, P, PACK], BF16, name="z_grouped%d" % b, tag="z_grouped%d" % b, align_bytes=64)
+            z_grouped[b] = keep.tile([P, P, PACK], BF16, name="z_grouped%d" % b, tag=pins.get("z_grouped%d" % b, "z_grouped%d" % b), align_bytes=64)
             nc.vector.tensor_tensor(
                 z_grouped[b][:], back[b][:].rearrange("p t j -> p j t"),
                 ga_sb[:].unsqueeze(1).to_broadcast([P, P, PACK]), ALU.mult,
@@ -248,7 +261,7 @@ def tile_picked_selfegcemoebz_none_p_kernel(
 
         def quantise(b):
             z_codes[b] = keep.tile([P, P], U32, name="z_codes%d" % b, tag="z_codes%d" % b, align_bytes=64)
-            z_scale[b] = keep.tile([P, P], U8, name="z_scale%d" % b, align_bytes=64)
+            z_scale[b] = keep.tile([P, P], U8, name="z_scale%d" % b, tag="z_scale%d" % b, align_bytes=64)
             nc.vector.quantize_mx(
                 out=z_codes[b][:].bitcast(FP8X4), scales=z_scale[b][:],
                 in_=z_grouped[b][:].rearrange("p j t -> p (j t)"),
@@ -269,10 +282,10 @@ def tile_picked_selfegcemoebz_none_p_kernel(
 
         def leave_bank(b):
             acc = s_acc[b]
-            low = keep.tile([P, 1], F32, name="low%d" % b)
+            low = keep.tile([P, 1], F32, name="low%d" % b, tag="low%d" % b, align_bytes=64)
             nc.vector.tensor_scalar(s_win[b][:, :S], acc[:], 0.0625, None, ALU.mult, ALU.min, accum_out=low[:])
             exp_bias[b] = keep.tile([P, 1], F32, name="exp_bias%d" % b)
-            nc.gpsimd.tensor_tensor(exp_bias[b][:], low[:], tau_sb[:, b : b + 1], ALU.mult)
+            (nc.vector if b in (2, 3) else nc.gpsimd).tensor_tensor(exp_bias[b][:], low[:], tau_sb[:, b : b + 1], ALU.mult)
 
         fetched = {}
 
@@ -283,6 +296,29 @@ def tile_picked_selfegcemoebz_none_p_kernel(
             else:
                 nc.vector.tensor_copy(fetched[b][:], s_win[b][:].indirect(n5_sb[:]))
 
+        last = BLOCKS - 1
+        last_larger = keep.tile([P, PACK, P], F32, name="last_larger")
+
+        def compare_last(t):
+            terms = sg[last, t].rearrange("p (j u) -> p j u", u=MEMBERS)
+            y_block = y_win[t][:, last * P : (last + 1) * P]
+            count_t = keep.tile([P, P], F32, name="last_count%d" % t, tag=pins.get("last_count%d" % t, "last_count%d" % t), align_bytes=64)
+            if t == PACK - 1:
+                nc.vector.tensor_reduce(count_t[:], terms, mybir.AxisListType.X, ALU.add)
+                nc.vector.scalar_tensor_tensor(last_larger[:, t, :], count_t[:], -1.5, y_block, ALU.add, ALU.max)
+            else:
+                halves = pairs[last * PACK + t][0]
+                nc.gpsimd.tensor_tensor(halves, terms[:, :, 0:2], terms[:, :, 2:4], ALU.add)
+                nc.vector.scalar_tensor_tensor(count_t[:], halves[:, :, 0], -1.5, halves[:, :, 1], ALU.add, ALU.add)
+                nc.vector.tensor_tensor(last_larger[:, t, :], count_t[:], y_block, ALU.max)
+
+        def weigh_last():
+            z_grouped[last] = keep.tile([P, P, PACK], BF16, name="z_grouped%d" % last, tag=pins.get("z_grouped3", "z_grouped3"), align_bytes=64)
+            nc.vector.tensor_tensor(
+                z_grouped[last][:], last_larger[:].rearrange("p t j -> p j t"),
+                ga_sb[:].unsqueeze(1).to_broadcast([P, P, PACK]), ALU.mult,
+            )
+
         def block_members(b, ts):
             for t in ts:
                 members(b, t)
@@ -292,10 +328,6 @@ def tile_picked_selfegcemoebz_none_p_kernel(
         gate2(1)
         gate2(2)
         gate2(3)
-        turn_y(0)
-        turn_y(1)
-        turn_y(2)
-        turn_y(3)
         members(0, 0)
         members(0, 1)
         members(0, 2)
@@ -312,6 +344,19 @@ def tile_picked_selfegcemoebz_none_p_kernel(
         members(3, 1)
         members(3, 2)
         members(3, 3)
+        fetch3(0)
+        apply_gate(0)
+        turn_y(0)
+        compare2(0)
+        weigh2(0)
+        fetch3(1)
+        apply_gate(1)
+        turn_y(1)
+        compare2(1)
+        weigh2(1)
+        fetch3(2)
+        apply_gate(2)
+        turn_y(2)
         count(0, 0)
         count(0, 1)
         count(0, 2)
@@ -320,76 +365,63 @@ def tile_picked_selfegcemoebz_none_p_kernel(
         count(1, 1)
         count(1, 2)
         count(1, 3)
-        count(2, 0)
-        fetch3(0)
-        apply_gate(0)
-        fetch3(1)
-        compare2(0)
-        apply_gate(1)
-        weigh2(0)
-        fetch3(2)
-        compare2(1)
-        apply_gate(2)
-        weigh2(1)
-        fetch3(3)
         compare2(2)
-        apply_gate(3)
         weigh2(2)
-        compare2(3)
+        fetch3(3)
+        apply_gate(3)
         compare(0)
         turn_back(0)
+        compare2(3)
         weigh2(3)
         group2()
-        count(2, 1)
-        count(2, 2)
-        count(2, 3)
         quantise2()
         compare(1)
         turn_back(1)
         weigh(0)
-        weigh(1)
         quantise(0)
         second_product(0)
-        count(3, 0)
-        count(3, 1)
+        count(2, 0)
+        count(2, 1)
+        count(2, 2)
+        count(2, 3)
+        weigh(1)
+        leave_bank(0)
         quantise(1)
         second_product(1)
-        leave_bank(0)
+        fetch5(0, "vector")
+        leave_bank(1)
         compare(2)
         turn_back(2)
-        count(3, 2)
-        count(3, 3)
-        leave_bank(1)
-        fetch5(0, "vector")
+        compare_last(0)
         weigh(2)
+        compare_last(1)
         quantise(2)
         second_product(2)
-        compare(3)
-        turn_back(3)
+        compare_last(3)
+        compare_last(2)
+        weigh_last()
         leave_bank(2)
-        weigh(3)
         quantise(3)
         second_product(3)
 
         ea = keep.tile([P, BLOCKS, S], F32, name="ea")
 
-        def decay(b):
+        def decay(b, lo=0, hi=S):
             nc.scalar.activation(
-                ea[:, b, :], s_win[b][:].indirect(n4_sb[:]), ACT.Exp,
+                ea[:, b, lo:hi], s_win[b][:].indirect(n4_sb[:, lo // 16 : hi // 16]), ACT.Exp,
                 bias=exp_bias[b][:], scale=neg_tau[:, b : b + 1],
             )
 
+        weighted = keep.tile([P, BLOCKS, S], F32, name="weighted", tag=pins.get("weighted", "z_grouped3"), align_bytes=64)
 
-        weighted = keep.tile([P, BLOCKS, S], F32, name="weighted", tag="z_grouped%d" % (BLOCKS - 1), align_bytes=64)
+        def weight5(b, lo=0, hi=S):
+            s5 = fetched[b][:, lo:hi] if b in fetched else s_win[b][:].indirect(n5_sb[:])
+            nc.vector.tensor_tensor(weighted[:, b, lo:hi], s5, ea[:, b, lo:hi], ALU.mult)
 
-        def weight5(b):
-            s5 = fetched[b][:] if b in fetched else s_win[b][:].indirect(n5_sb[:])
-            nc.vector.tensor_tensor(weighted[:, b, :], s5, ea[:, b, :], ALU.mult)
-
-        def finish(b):
-            result = keep.tile([P, S], F32, name="result%d" % b)
-            nc.vector.scalar_tensor_tensor(result[:], weighted[:, b, :], -2.0, s_win[b][:, :S], ALU.mult, ALU.add)
-            nc.sync.dma_start(out=out[b * P : (b + 1) * P, :], in_=result[:])
+        def finish(b, lo=0, hi=S):
+            result = keep.tile([P, hi - lo], F32, name="result%d_%d" % (b, lo))
+            nc.vector.scalar_tensor_tensor(result[:], weighted[:, b, lo:hi], -2.0, s_win[b][:, lo:hi], ALU.mult, ALU.add)
+            nc.sync.dma_start(out=out[b * P : (b + 1) * P, lo:hi], in_=result[:])
 
         decay(0)
         decay(1)
@@ -397,12 +429,15 @@ def tile_picked_selfegcemoebz_none_p_kernel(
         fetch5(2, "scalar")
         weight5(0)
         leave_bank(3)
-        decay(3)
         fetch5(3, "scalar")
+        decay(3, 0, HALF)
+        decay(3, HALF, S)
         finish(0)
         weight5(1)
         weight5(2)
         finish(1)
         finish(2)
-        weight5(3)
-        finish(3)
+        weight5(3, 0, HALF)
+        weight5(3, HALF, S)
+        finish(3, 0, HALF)
+        finish(3, HALF, S)

@@ -19,11 +19,15 @@ P = 128
 PACK = 4
 T = 2048
 S = 512
+HALF = S // 2
 MEMBERS = 4
 BLOCKS = S // P
+LAST = BLOCKS - 1
+LAST_TILE = PACK - 1
 WINDOW = 2 * S
-LIST_COLS = S // 16
-HALF = S // 2
+PER_COLUMN = 16
+PRODUCT_BANKS = 4
+COUNT_BANKS = 3
 
 
 def tile_picked_selfegcemoebz_none_p_kernel(
@@ -33,6 +37,12 @@ def tile_picked_selfegcemoebz_none_p_kernel(
     with ExitStack() as ctx:
         keep = ctx.enter_context(tc.tile_pool(name="keep", bufs=1))
         psum = ctx.enter_context(tc.psum_pool(name="psum", bufs=1))
+
+        def scratch(name, shape, dtype, after=None):
+            return keep.tile(shape, dtype, name=name, tag=after or name, align_bytes=64)
+
+        def entries(list_tile, first, stop):
+            return list_tile[:, first // PER_COLUMN : stop // PER_COLUMN]
 
         def load_list(name, src):
             tile = keep.tile(list(src.shape), U16, name=name)
@@ -44,6 +54,13 @@ def tile_picked_selfegcemoebz_none_p_kernel(
             queue.dma_start(out=tile[:], in_=src.rearrange("(p t) o -> p (t o)", t=PACK))
             return tile
 
+        def sigmoid_bias(name, slope, threshold):
+            product = keep.tile([P, PACK], F32, name=name + "_product")
+            nc.gpsimd.tensor_tensor(product[:], slope[:], threshold[:], ALU.mult)
+            bias = keep.tile([P, PACK], F32, name=name)
+            nc.gpsimd.tensor_scalar(bias[:], product[:], -1.0, 0.0, ALU.mult, ALU.add)
+            return bias
+
         warm_in = keep.tile([P, 1], F32, name="warm_in")
         warm_out = keep.tile([P, 1], F32, name="warm_out")
         nc.vector.memset(warm_in[:], 0.0)
@@ -52,28 +69,20 @@ def tile_picked_selfegcemoebz_none_p_kernel(
         scale_table = keep.tile([P, T], U8, name="scale_table")
         nc.gpsimd.memset(scale_table[:].bitcast(I32), 0)
         w_rows = w1.rearrange("(p j) c -> p j c", j=PACK)
-        w_raw = [keep.tile([P, PACK, S // 2], F32, name="w_raw%d" % h) for h in range(2)]
-        nc.sync.dma_start(out=w_raw[0][:], in_=w_rows[:, :, : S // 2])
+        w_raw = [keep.tile([P, PACK, HALF], F32, name="w_raw%d" % h) for h in range(2)]
+        nc.sync.dma_start(out=w_raw[0][:], in_=w_rows[:, :, :HALF])
         offs_sb = load_list("offs_sb", offs)
         for q in range(4):
             nc.sync.dma_start(
                 out=scale_table[32 * q : 32 * q + 4, :].bitcast(I32),
                 in_=x_scales[0, 4 * q : 4 * q + 4, :].bitcast(I32),
             )
-        nc.sync.dma_start(out=w_raw[1][:], in_=w_rows[:, :, S // 2 :])
+        nc.sync.dma_start(out=w_raw[1][:], in_=w_rows[:, :, HALF:])
         word_table = keep.tile([P, T], U32, name="word_table")
         nc.sync.dma_start(
             out=word_table[:].bitcast(I32),
             in_=x_words[0].rearrange("p n r -> p (n r)").bitcast(I32),
         )
-
-        def sigmoid_bias(name, slope, threshold):
-            product = keep.tile([P, PACK], F32, name=name + "_product")
-            nc.gpsimd.tensor_tensor(product[:], slope[:], threshold[:], ALU.mult)
-            bias = keep.tile([P, PACK], F32, name=name)
-            nc.gpsimd.tensor_scalar(bias[:], product[:], -1.0, 0.0, ALU.mult, ALU.add)
-            return bias
-
         n2_sb = load_list("n2_sb", n2)
         sl2_sb = load_by_feature("sl2_sb", sl2, nc.gpsimd)
         th2_sb = load_by_feature("th2_sb", th2, nc.gpsimd)
@@ -84,7 +93,7 @@ def tile_picked_selfegcemoebz_none_p_kernel(
         gb_sb = load_by_feature("gb_sb", gb, nc.sync)
         ga_sb = load_by_feature("ga_sb", ga, nc.sync)
         tau_sb = keep.tile([P, BLOCKS], F32, name="tau_sb")
-        with nc.allow_non_contiguous_dma(reason="one value of tau a partition and block"):
+        with nc.allow_non_contiguous_dma(reason="row 128 b + p of s lies on partition p of block b"):
             nc.sync.dma_start(out=tau_sb[:], in_=tau.rearrange("(b p) o -> p (b o)", p=P))
         n4_sb = load_list("n4_sb", n4)
         n5_sb = load_list("n5_sb", n5)
@@ -94,102 +103,96 @@ def tile_picked_selfegcemoebz_none_p_kernel(
         bias1 = sigmoid_bias("bias1", sl_sb, th_sb)
         neg_tau = keep.tile([P, BLOCKS], F32, name="neg_tau")
         nc.gpsimd.tensor_scalar(neg_tau[:], tau_sb[:], -1.0, 0.0, ALU.mult, ALU.add)
+        ga_by_column = ga_sb[:].unsqueeze(1).to_broadcast([P, P, PACK])
 
         y_win = [keep.tile([P, WINDOW], F32, name="y_win%d" % t) for t in range(PACK)]
         s_win = [keep.tile([P, WINDOW], F32, name="s_win%d" % b) for b in range(BLOCKS)]
+        sg2 = [win[:, S:] for win in s_win]
         for win in y_win:
             nc.vector.memset(win[:, S:], 0.0)
 
-        w_grouped = keep.tile([P, PACK, P, PACK], BF16, name="w_grouped", align_bytes=64)
+        w_grouped = scratch("w_grouped", [P, PACK, P, PACK], BF16)
         for h, cast in enumerate((nc.scalar.copy, nc.vector.tensor_copy)):
             cast(
                 w_grouped[:, :, h * (P // 2) : (h + 1) * (P // 2), :],
                 w_raw[h][:].rearrange("p j (m t) -> p t m j", t=PACK),
             )
-        x_scale = keep.tile([P, S], U8, name="x_scale", align_bytes=64)
+        x_scale = scratch("x_scale", [P, S], U8)
         nc.vector.tensor_copy(x_scale[:], scale_table[:].indirect(offs_sb[:]))
-        w_codes = keep.tile([P, S], U32, name="w_codes", align_bytes=64)
-        w_scale = keep.tile([P, S], U8, name="w_scale", align_bytes=64)
+        w_codes = scratch("w_codes", [P, S], U32)
+        w_scale = scratch("w_scale", [P, S], U8)
         nc.vector.quantize_mx(
             out=w_codes[:].bitcast(FP8X4),
             scales=w_scale[:],
             in_=w_grouped[:].rearrange("p t m j -> p (t m j)"),
         )
-        x_codes = keep.tile([P, S], U32, name="x_codes", align_bytes=64)
-        for h in range(2):
+        x_codes = scratch("x_codes", [P, S], U32)
+        for first in (0, HALF):
             nc.vector.tensor_copy(
-                x_codes[:, h * HALF : (h + 1) * HALF],
-                word_table[:].indirect(offs_sb[:, h * LIST_COLS // 2 : (h + 1) * LIST_COLS // 2]),
+                x_codes[:, first : first + HALF],
+                word_table[:].indirect(entries(offs_sb, first, first + HALF)),
             )
 
-        def first_product(t, cols, leave, tag, bufs):
-            feats = slice(t * P, (t + 1) * P)
-            acc = psum.tile([P, cols.stop - cols.start], F32, name="y_acc%d_%d" % (t, cols.start), tag=tag, bufs=bufs)
+        def product_bank(name, shape):
+            return psum.tile(shape, F32, name=name, tag="product", bufs=PRODUCT_BANKS)
+
+        def turning_bank(name, shape):
+            return psum.tile(shape, F32, name=name, tag="turning")
+
+        def first_product(t, first, stop, bank, copy):
+            features = slice(t * P, (t + 1) * P)
+            acc = bank("y_acc%d_%d" % (t, first), [P, stop - first])
             nc.tensor.matmul_mx(
                 out=acc[:],
-                lhsT=w_codes[:, feats].bitcast(FP8X4),
-                lhsT_scale=w_scale[:, feats],
-                rhs=x_codes[:, cols].bitcast(FP8X4),
-                rhs_scale=x_scale[:, cols],
+                lhsT=w_codes[:, features].bitcast(FP8X4),
+                lhsT_scale=w_scale[:, features],
+                rhs=x_codes[:, first:stop].bitcast(FP8X4),
+                rhs_scale=x_scale[:, first:stop],
                 start=True,
                 stop=True,
             )
-            leave(y_win[t][:, cols], acc[:])
+            copy(y_win[t][:, first:stop], acc[:])
 
-        first_product(0, slice(0, HALF), nc.scalar.copy, "turn", 1)
-        first_product(0, slice(HALF, S), nc.scalar.copy, "product", 4)
+        first_product(0, 0, HALF, turning_bank, nc.scalar.copy)
+        first_product(0, HALF, S, product_bank, nc.scalar.copy)
         for t in range(1, PACK):
-            first_product(t, slice(0, S), nc.vector.tensor_copy, "product", 4)
+            first_product(t, 0, S, product_bank, nc.vector.tensor_copy)
 
-        sg2, sg, y3, gated, larger2, y_turned, larger, z_grouped, s_acc, exp_bias = ({} for k in range(10))
-
-        def gate2(t):
-            sg2[t] = keep.tile([P, S], F32, name="sg2_%d" % t, tag="sg2_%d" % t, align_bytes=64)
+        for t in range(PACK):
             nc.scalar.activation(
-                sg2[t][:], y_win[t][:].indirect(n2_sb[:]), ACT.Sigmoid,
+                sg2[t], y_win[t][:].indirect(n2_sb[:]), ACT.Sigmoid,
                 bias=bias2[:, t : t + 1], scale=sl2_sb[:, t : t + 1],
             )
+        sg = {}
+        for b in range(BLOCKS):
+            for t in range(PACK):
+                tile = scratch("sg%d_%d" % (b, t), [P, S], F32)
+                nc.scalar.activation(
+                    tile[:], y_win[t][:].indirect(entries(n1_sb, b * S, (b + 1) * S)), ACT.Sigmoid,
+                    bias=bias1[:, t : t + 1], scale=sl_sb[:, t : t + 1],
+                )
+                sg[b, t] = tile[:].rearrange("p (j u) -> p j u", u=MEMBERS)
 
-        held = {}
-        pins = {"larger0": "sg2_3", "larger1": "z2_grouped", "z_grouped0": "z2_rows", "last_count3": "z_grouped2", "s5_0": "z_grouped1"}
-        reused = {}
+        y3, gated, larger2 = {}, {}, {}
+        z2_rows = scratch("z2_rows", [P, PACK, S], BF16)
+        z2_grouped = scratch("z2_grouped", [P, S, PACK], BF16)
+        z2_codes = scratch("z2_codes", [P, S], U32)
+        z2_scale = scratch("z2_scale", [P, S], U8)
 
-        def members(b, t):
-            chunk = b * PACK + t
-            if chunk not in held:
-                name = "sg_%d" % chunk
-                tag, n = reused.get(chunk, (name, 1))
-                tile = keep.tile([P, n * S], F32, name=name, tag=tag, align_bytes=64)
-                for k in range(n):
-                    held[chunk + k] = tile[:, k * S : (k + 1) * S]
-            sg[b, t] = held[chunk]
-            nc.scalar.activation(
-                sg[b, t],
-                y_win[t][:].indirect(n1_sb[:, b * LIST_COLS : (b + 1) * LIST_COLS]),
-                ACT.Sigmoid,
-                bias=bias1[:, t : t + 1], scale=sl_sb[:, t : t + 1],
-            )
+        def apply_gate(t, after=None):
+            gated[t] = scratch("gated%d" % t, [P, S], F32, after)
+            nc.gpsimd.tensor_tensor(gated[t][:], y_win[t][:, :S], sg2[t], ALU.mult)
 
         def fetch3(t):
-            y3[t] = keep.tile([P, S], F32, name="y3_%d" % t, tag="y3_%d" % t, align_bytes=64)
+            y3[t] = scratch("y3_%d" % t, [P, S], F32)
             nc.vector.tensor_copy(y3[t][:], y_win[t][:].indirect(n3_sb[:]))
 
-        def apply_gate(t):
-            gated[t] = s_win[t][:, S:]
-            nc.vector.tensor_tensor(gated[t], y_win[t][:, :S], sg2[t][:], ALU.mult)
-
         def compare2(t):
-            larger2[t] = keep.tile([P, S], F32, name="larger2_%d" % t, tag="larger2_%d" % t, align_bytes=64)
-            nc.vector.scalar_tensor_tensor(larger2[t][:], y3[t][:], 0.75, gated[t], ALU.mult, ALU.max)
+            larger2[t] = scratch("larger2_%d" % t, [P, S], F32)
+            nc.vector.scalar_tensor_tensor(larger2[t][:], y3[t][:], 0.75, gated[t][:], ALU.mult, ALU.max)
 
-        z2_rows = keep.tile([P, PACK, S], BF16, name="z2_rows", tag="z2_rows", align_bytes=64)
-
-        def weigh2(t):
-            (nc.gpsimd if t in (0, 1, 2) else nc.vector).tensor_scalar(z2_rows[:, t, :], larger2[t][:], gb_sb[:, t : t + 1], 0.0, ALU.mult, ALU.add)
-
-        z2_grouped = keep.tile([P, S, PACK], BF16, name="z2_grouped", tag="z2_grouped", align_bytes=64)
-        z2_codes = keep.tile([P, S], U32, name="z2_codes", align_bytes=64)
-        z2_scale = keep.tile([P, S], U8, name="z2_scale", align_bytes=64)
+        def weigh2(t, engine):
+            engine.tensor_scalar(z2_rows[:, t, :], larger2[t][:], gb_sb[:, t : t + 1], 0.0, ALU.mult, ALU.add)
 
         def group2():
             nc.vector.tensor_copy(
@@ -203,32 +206,29 @@ def tile_picked_selfegcemoebz_none_p_kernel(
                 in_=z2_grouped[:].rearrange("p c t -> p (c t)"),
             )
 
+        y_turned, cnt, larger, back, z_grouped, z_codes, z_scale, s_acc, exp_bias = ({} for name in range(9))
+
         def turn_y(b):
-            turn = psum.tile([P, PACK, P], F32, name="y_turn%d" % b, tag="product", bufs=4)
+            turn = product_bank("y_turn%d" % b, [P, PACK, P])
             for t in range(PACK):
                 nc.tensor.transpose(turn[:, t, :], y_win[t][:, b * P : (b + 1) * P], ident[:])
-            y_turned[b] = keep.tile([P, S], F32, name="y_turned%d" % b, tag="y_turned%d" % b, align_bytes=64)
+            y_turned[b] = scratch("y_turned%d" % b, [P, S], F32)
             nc.vector.tensor_copy(y_turned[b][:], turn[:].rearrange("j t p -> j (t p)"))
 
-        cnt = {}
-        pairs = {}
-        paired = {8: ("y_turned1", 7, nc.gpsimd)}
+        def pair_tile(name, n, after):
+            tile = scratch(name, [P, n * 2 * P], F32, after)
+            return tile[:].rearrange("p (j u) -> p j u", u=2)
 
-        def count(b, t):
+        def add_pairs(engine, pairs, b, t):
+            engine.tensor_tensor(pairs, sg[b, t][:, :, 0:2], sg[b, t][:, :, 2:4], ALU.add)
+
+        def count(b, t, pairs=None):
             if t == 0:
-                if True:
-                    cnt[b] = psum.tile([P, PACK, P], F32, name="cnt%d" % b, tag="cnt", bufs=3)
-            terms = sg[b, t].rearrange("p (j u) -> p j u", u=MEMBERS)
-            chunk = b * PACK + t
-            if chunk in paired:
-                tag, n, engine = paired[chunk]
-                tile = keep.tile([P, n * 2 * P], F32, name="pairs%d" % chunk, tag=tag or "pairs%d" % chunk, align_bytes=64)
-                for k in range(n):
-                    pairs[chunk + k] = (tile[:, k * 2 * P : (k + 1) * 2 * P].rearrange("p (j u) -> p j u", u=2), engine)
-            if chunk in pairs:
-                halves, engine = pairs[chunk]
-                engine.tensor_tensor(halves, terms[:, :, 0:2], terms[:, :, 2:4], ALU.add)
-                terms = halves
+                cnt[b] = psum.tile([P, PACK, P], F32, name="cnt%d" % b, tag="cnt", bufs=COUNT_BANKS)
+            terms = sg[b, t]
+            if pairs is not None:
+                add_pairs(nc.vector, pairs, b, t)
+                terms = pairs
             n = terms.shape[2]
             for u in range(n):
                 nc.tensor.matmul(
@@ -236,41 +236,30 @@ def tile_picked_selfegcemoebz_none_p_kernel(
                     start=(u == 0), stop=(u == n - 1), is_transpose=True,
                 )
 
-        def compare(b):
-            larger[b] = keep.tile([P, PACK, P], F32, name="larger%d" % b, tag=pins.get("larger%d" % b, "larger%d" % b), align_bytes=64)
+        def compare(b, after=None):
+            larger[b] = scratch("larger%d" % b, [P, PACK, P], F32, after)
             nc.vector.scalar_tensor_tensor(
                 larger[b][:].rearrange("j t p -> j (t p)"), cnt[b][:].rearrange("j t p -> j (t p)"), -1.5,
                 y_turned[b][:], ALU.add, ALU.max,
             )
-
-        back = {}
-
-        def turn_back(b):
-            back[b] = psum.tile([P, PACK, P], F32, name="back%d" % b, tag="turn", bufs=1)
+            back[b] = turning_bank("back%d" % b, [P, PACK, P])
             for t in range(PACK):
                 nc.tensor.transpose(back[b][:, t, :], larger[b][:, t, :], ident[:])
 
-        def weigh(b):
-            z_grouped[b] = keep.tile([P, P, PACK], BF16, name="z_grouped%d" % b, tag=pins.get("z_grouped%d" % b, "z_grouped%d" % b), align_bytes=64)
-            nc.vector.tensor_tensor(
-                z_grouped[b][:], back[b][:].rearrange("p t j -> p j t"),
-                ga_sb[:].unsqueeze(1).to_broadcast([P, P, PACK]), ALU.mult,
-            )
+        def weigh(b, after=None):
+            z_grouped[b] = scratch("z_grouped%d" % b, [P, P, PACK], BF16, after)
+            nc.vector.tensor_tensor(z_grouped[b][:], back[b][:].rearrange("p t j -> p j t"), ga_by_column, ALU.mult)
 
-        z_codes, z_scale = {}, {}
-
-        def quantise(b):
-            z_codes[b] = keep.tile([P, P], U32, name="z_codes%d" % b, tag="z_codes%d" % b, align_bytes=64)
-            z_scale[b] = keep.tile([P, P], U8, name="z_scale%d" % b, tag="z_scale%d" % b, align_bytes=64)
+        def second_product(b):
+            z_codes[b] = scratch("z_codes%d" % b, [P, P], U32)
+            z_scale[b] = scratch("z_scale%d" % b, [P, P], U8)
             nc.vector.quantize_mx(
                 out=z_codes[b][:].bitcast(FP8X4), scales=z_scale[b][:],
                 in_=z_grouped[b][:].rearrange("p j t -> p (j t)"),
             )
-
-        def second_product(b):
-            acc = psum.tile([P, S], F32, name="s_acc%d" % b, tag="product", bufs=4)
+            s_acc[b] = product_bank("s_acc%d" % b, [P, S])
             nc.tensor.matmul_mx(
-                out=acc[:],
+                out=s_acc[b][:],
                 lhsT=z_codes[b][:].bitcast(FP8X4),
                 lhsT_scale=z_scale[b][:],
                 rhs=z2_codes[:].bitcast(FP8X4),
@@ -278,166 +267,125 @@ def tile_picked_selfegcemoebz_none_p_kernel(
                 start=True,
                 stop=True,
             )
-            s_acc[b] = acc
 
-        def leave_bank(b):
-            acc = s_acc[b]
-            low = keep.tile([P, 1], F32, name="low%d" % b, tag="low%d" % b, align_bytes=64)
-            nc.vector.tensor_scalar(s_win[b][:, :S], acc[:], 0.0625, None, ALU.mult, ALU.min, accum_out=low[:])
+        def leave_bank(b, engine):
+            low = scratch("low%d" % b, [P, 1], F32)
+            nc.vector.tensor_scalar(s_win[b][:, :S], s_acc[b][:], 0.0625, None, ALU.mult, ALU.min, accum_out=low[:])
             exp_bias[b] = keep.tile([P, 1], F32, name="exp_bias%d" % b)
-            (nc.vector if b in (2, 3) else nc.gpsimd).tensor_tensor(exp_bias[b][:], low[:], tau_sb[:, b : b + 1], ALU.mult)
+            engine.tensor_tensor(exp_bias[b][:], low[:], tau_sb[:, b : b + 1], ALU.mult)
 
-        fetched = {}
+        s5 = {}
 
-        def fetch5(b, engine):
-            fetched[b] = keep.tile([P, S], F32, name="s5_%d" % b, tag=pins.get("s5_%d" % b, "s5_%d" % b), align_bytes=64)
-            if engine == "scalar":
-                nc.scalar.activation(fetched[b][:], s_win[b][:].indirect(n5_sb[:]), ACT.Copy)
-            else:
-                nc.vector.tensor_copy(fetched[b][:], s_win[b][:].indirect(n5_sb[:]))
+        def fetch5_on_vector(b, after):
+            s5[b] = scratch("s5_%d" % b, [P, S], F32, after)
+            nc.vector.tensor_copy(s5[b][:], s_win[b][:].indirect(n5_sb[:]))
 
-        last = BLOCKS - 1
-        last_larger = keep.tile([P, PACK, P], F32, name="last_larger")
+        def fetch5_on_scalar(b):
+            s5[b] = scratch("s5_%d" % b, [P, S], F32)
+            nc.scalar.activation(s5[b][:], s_win[b][:].indirect(n5_sb[:]), ACT.Copy)
 
-        def compare_last(t):
-            terms = sg[last, t].rearrange("p (j u) -> p j u", u=MEMBERS)
-            y_block = y_win[t][:, last * P : (last + 1) * P]
-            count_t = keep.tile([P, P], F32, name="last_count%d" % t, tag=pins.get("last_count%d" % t, "last_count%d" % t), align_bytes=64)
-            if t == PACK - 1:
-                nc.vector.tensor_reduce(count_t[:], terms, mybir.AxisListType.X, ALU.add)
-                nc.vector.scalar_tensor_tensor(last_larger[:, t, :], count_t[:], -1.5, y_block, ALU.add, ALU.max)
-            else:
-                halves = pairs[last * PACK + t][0]
-                nc.gpsimd.tensor_tensor(halves, terms[:, :, 0:2], terms[:, :, 2:4], ALU.add)
-                nc.vector.scalar_tensor_tensor(count_t[:], halves[:, :, 0], -1.5, halves[:, :, 1], ALU.add, ALU.add)
-                nc.vector.tensor_tensor(last_larger[:, t, :], count_t[:], y_block, ALU.max)
-
-        def weigh_last():
-            z_grouped[last] = keep.tile([P, P, PACK], BF16, name="z_grouped%d" % last, tag=pins.get("z_grouped3", "z_grouped3"), align_bytes=64)
-            nc.vector.tensor_tensor(
-                z_grouped[last][:], last_larger[:].rearrange("p t j -> p j t"),
-                ga_sb[:].unsqueeze(1).to_broadcast([P, P, PACK]), ALU.mult,
-            )
-
-        def block_members(b, ts):
-            for t in ts:
-                members(b, t)
-                count(b, t)
-
-        gate2(0)
-        gate2(1)
-        gate2(2)
-        gate2(3)
-        members(0, 0)
-        members(0, 1)
-        members(0, 2)
-        members(0, 3)
-        members(1, 0)
-        members(1, 1)
-        members(1, 2)
-        members(1, 3)
-        members(2, 0)
-        members(2, 1)
-        members(2, 2)
-        members(2, 3)
-        members(3, 0)
-        members(3, 1)
-        members(3, 2)
-        members(3, 3)
-        fetch3(0)
-        apply_gate(0)
+        for t in (0, 1):
+            apply_gate(t)
+        for t in (0, 1):
+            fetch3(t)
         turn_y(0)
-        compare2(0)
-        weigh2(0)
-        fetch3(1)
-        apply_gate(1)
-        turn_y(1)
-        compare2(1)
-        weigh2(1)
-        fetch3(2)
-        apply_gate(2)
-        turn_y(2)
-        count(0, 0)
-        count(0, 1)
-        count(0, 2)
-        count(0, 3)
-        count(1, 0)
-        count(1, 1)
-        count(1, 2)
-        count(1, 3)
-        compare2(2)
-        weigh2(2)
-        fetch3(3)
-        apply_gate(3)
-        compare(0)
-        turn_back(0)
-        compare2(3)
-        weigh2(3)
+        for t in (0, 1):
+            compare2(t)
+        apply_gate(2, after="y3_1")
+        apply_gate(3, after="gated0")
+        weigh2(0, nc.gpsimd)
+        for t in (2, 3):
+            fetch3(t)
+        for b in (1, 2):
+            turn_y(b)
+        for t in range(PACK):
+            count(0, t)
+        for t in (0, 1):
+            count(1, t)
+        for t in (2, 3):
+            compare2(t)
+        for t in (1, 2):
+            weigh2(t, nc.vector)
+        compare(0, after="y3_2")
+        weigh2(3, nc.vector)
         group2()
+
+        pairs = pair_tile("pairs1_late", 2, after="z2_rows")
+        for k, t in enumerate((2, 3)):
+            count(1, t, pairs[:, k * P : (k + 1) * P, :])
+        weigh(0, after="larger2_3")
         quantise2()
-        compare(1)
-        turn_back(1)
-        weigh(0)
-        quantise(0)
         second_product(0)
-        count(2, 0)
-        count(2, 1)
-        count(2, 2)
-        count(2, 3)
+        compare(1)
+        leave_bank(0, nc.gpsimd)
+        pairs = pair_tile("pairs2_early", 2, after="y_turned1")
+        count(2, 0, pairs[:, :P, :])
         weigh(1)
-        leave_bank(0)
-        quantise(1)
+        count(2, 1, pairs[:, P:, :])
         second_product(1)
-        fetch5(0, "vector")
-        leave_bank(1)
+        pairs = pair_tile("pairs2_late", 2, after="z_grouped1")
+        for k, t in enumerate((2, 3)):
+            count(2, t, pairs[:, k * P : (k + 1) * P, :])
+        leave_bank(1, nc.gpsimd)
+        last_pairs = pair_tile("last_pairs", LAST_TILE, after="z_codes1")
+        for t in range(LAST_TILE):
+            add_pairs(nc.gpsimd, last_pairs[:, t * P : (t + 1) * P, :], LAST, t)
         compare(2)
-        turn_back(2)
-        compare_last(0)
+        fetch5_on_vector(0, after="y_turned2")
         weigh(2)
-        compare_last(1)
-        quantise(2)
+
+        last_columns = slice(LAST * P, S)
+        back[LAST] = keep.tile([P, PACK, P], F32, name="last_larger")
+        last_cnt = scratch("last_cnt", [P, LAST_TILE * P], F32, after="larger2")
+        nc.vector.scalar_tensor_tensor(last_cnt[:], last_pairs[:, :, 0], -1.5, last_pairs[:, :, 1], ALU.add, ALU.add)
         second_product(2)
-        compare_last(3)
-        compare_last(2)
-        weigh_last()
-        leave_bank(2)
-        quantise(3)
-        second_product(3)
+        for t in range(LAST_TILE):
+            nc.vector.tensor_tensor(
+                back[LAST][:, t, :], last_cnt[:, t * P : (t + 1) * P], y_win[t][:, last_columns], ALU.max
+            )
+        final_cnt = scratch("final_cnt", [P, P], F32, after="z_grouped2")
+        nc.vector.tensor_reduce(final_cnt[:], sg[LAST, LAST_TILE], mybir.AxisListType.X, ALU.add)
+        nc.vector.scalar_tensor_tensor(
+            back[LAST][:, LAST_TILE, :], final_cnt[:], -1.5, y_win[LAST_TILE][:, last_columns], ALU.add, ALU.max
+        )
+        leave_bank(2, nc.vector)
+        weigh(LAST)
+        second_product(LAST)
 
         ea = keep.tile([P, BLOCKS, S], F32, name="ea")
+        weighted = scratch("weighted", [P, BLOCKS, S], F32, after="z_grouped%d" % LAST)
 
-        def decay(b, lo=0, hi=S):
+        def decay(b, first=0, stop=S):
             nc.scalar.activation(
-                ea[:, b, lo:hi], s_win[b][:].indirect(n4_sb[:, lo // 16 : hi // 16]), ACT.Exp,
+                ea[:, b, first:stop], s_win[b][:].indirect(entries(n4_sb, first, stop)), ACT.Exp,
                 bias=exp_bias[b][:], scale=neg_tau[:, b : b + 1],
             )
 
-        weighted = keep.tile([P, BLOCKS, S], F32, name="weighted", tag=pins.get("weighted", "z_grouped3"), align_bytes=64)
+        def weight5(b, first=0, stop=S):
+            looked_up = s5[b][:, first:stop] if b in s5 else s_win[b][:].indirect(n5_sb[:])
+            nc.vector.tensor_tensor(weighted[:, b, first:stop], looked_up, ea[:, b, first:stop], ALU.mult)
 
-        def weight5(b, lo=0, hi=S):
-            s5 = fetched[b][:, lo:hi] if b in fetched else s_win[b][:].indirect(n5_sb[:])
-            nc.vector.tensor_tensor(weighted[:, b, lo:hi], s5, ea[:, b, lo:hi], ALU.mult)
+        def finish(b, first=0, stop=S):
+            result = keep.tile([P, stop - first], F32, name="result%d_%d" % (b, first))
+            nc.vector.scalar_tensor_tensor(
+                result[:], weighted[:, b, first:stop], -2.0, s_win[b][:, first:stop], ALU.mult, ALU.add
+            )
+            nc.sync.dma_start(out=out[b * P : (b + 1) * P, first:stop], in_=result[:])
 
-        def finish(b, lo=0, hi=S):
-            result = keep.tile([P, hi - lo], F32, name="result%d_%d" % (b, lo))
-            nc.vector.scalar_tensor_tensor(result[:], weighted[:, b, lo:hi], -2.0, s_win[b][:, lo:hi], ALU.mult, ALU.add)
-            nc.sync.dma_start(out=out[b * P : (b + 1) * P, lo:hi], in_=result[:])
-
-        decay(0)
-        decay(1)
-        decay(2)
-        fetch5(2, "scalar")
+        for b in range(LAST):
+            decay(b)
+        fetch5_on_scalar(2)
         weight5(0)
-        leave_bank(3)
-        fetch5(3, "scalar")
-        decay(3, 0, HALF)
-        decay(3, HALF, S)
+        leave_bank(LAST, nc.vector)
+        fetch5_on_scalar(LAST)
+        for first in (0, HALF):
+            decay(LAST, first, first + HALF)
         finish(0)
-        weight5(1)
-        weight5(2)
-        finish(1)
-        finish(2)
-        weight5(3, 0, HALF)
-        weight5(3, HALF, S)
-        finish(3, 0, HALF)
-        finish(3, HALF, S)
+        for b in (1, 2):
+            weight5(b)
+        for b in (1, 2):
+            finish(b)
+        for first in (0, HALF):
+            weight5(LAST, first, first + HALF)
+        for first in (0, HALF):
+            finish(LAST, first, first + HALF)

@@ -49,9 +49,9 @@ def tile_picked_selfegcemoebz_none_p_kernel(
             nc.sync.dma_start(tile[:], src)
             return tile
 
-        def load_by_feature(name, src, queue):
+        def load_by_feature(name, src):
             tile = keep.tile([P, PACK], F32, name=name)
-            queue.dma_start(out=tile[:], in_=src.rearrange("(p t) o -> p (t o)", t=PACK))
+            nc.sync.dma_start(out=tile[:], in_=src.rearrange("(p t) o -> p (t o)", t=PACK))
             return tile
 
         def sigmoid_bias(name, slope, threshold):
@@ -83,15 +83,15 @@ def tile_picked_selfegcemoebz_none_p_kernel(
             out=word_table[:].bitcast(I32),
             in_=x_words[0].rearrange("p n r -> p (n r)").bitcast(I32),
         )
+        sl2_sb = load_by_feature("sl2_sb", sl2)
+        th2_sb = load_by_feature("th2_sb", th2)
         n2_sb = load_list("n2_sb", n2)
-        sl2_sb = load_by_feature("sl2_sb", sl2, nc.gpsimd)
-        th2_sb = load_by_feature("th2_sb", th2, nc.gpsimd)
         n3_sb = load_list("n3_sb", n3)
         n1_sb = load_list("n1_sb", n1)
-        sl_sb = load_by_feature("sl_sb", sl, nc.sync)
-        th_sb = load_by_feature("th_sb", th, nc.sync)
-        gb_sb = load_by_feature("gb_sb", gb, nc.sync)
-        ga_sb = load_by_feature("ga_sb", ga, nc.sync)
+        sl_sb = load_by_feature("sl_sb", sl)
+        th_sb = load_by_feature("th_sb", th)
+        gb_sb = load_by_feature("gb_sb", gb)
+        ga_sb = load_by_feature("ga_sb", ga)
         tau_sb = keep.tile([P, BLOCKS], F32, name="tau_sb")
         with nc.allow_non_contiguous_dma(reason="row 128 b + p of s lies on partition p of block b"):
             nc.sync.dma_start(out=tau_sb[:], in_=tau.rearrange("(b p) o -> p (b o)", p=P))

from contextlib import ExitStack

import concourse.mybir as mybir
from concourse.masks import make_identity

FLOPS = 2 * 2 * 512 * 512 * 512

F32 = mybir.dt.float32
BF16 = mybir.dt.bfloat16
I32 = mybir.dt.int32
U32 = mybir.dt.uint32
U16 = mybir.dt.uint16
U8 = mybir.dt.uint8
FP8X4 = mybir.dt.float8_e4m3fn_x4
ALU = mybir.AluOpType
ACT = mybir.ActivationFunctionType

P = 128
PACK = 4
T = 2048
S = 512
HALF = S // 2
MEMBERS = 4
BLOCKS = S // P
LAST = BLOCKS - 1
LAST_TILE = PACK - 1
WINDOW = 2 * S
PER_COLUMN = 16
PRODUCT_BANKS = 4
COUNT_BANKS = 3


def tile_picked_selfegcemoebz_none_p_kernel(
    tc, x_words, x_scales, w1, sl, th, sl2, th2, ga, gb, tau, offs, n1, n2, n3, n4, n5, out
):
    nc = tc.nc
    with ExitStack() as ctx:
        keep = ctx.enter_context(tc.tile_pool(name="keep", bufs=1))
        psum = ctx.enter_context(tc.psum_pool(name="psum", bufs=1))

        def scratch(name, shape, dtype, after=None):
            return keep.tile(shape, dtype, name=name, tag=after or name, align_bytes=64)

        def entries(list_tile, first, stop):
            return list_tile[:, first // PER_COLUMN : stop // PER_COLUMN]

        def load_list(name, src):
            tile = keep.tile(list(src.shape), U16, name=name)
            nc.sync.dma_start(tile[:], src)
            return tile

        def load_by_feature(name, src):
            tile = keep.tile([P, PACK], F32, name=name)
            nc.sync.dma_start(out=tile[:], in_=src.rearrange("(p t) o -> p (t o)", t=PACK))
            return tile

        def sigmoid_bias(name, slope, threshold):
            product = keep.tile([P, PACK], F32, name=name + "_product")
            nc.gpsimd.tensor_tensor(product[:], slope[:], threshold[:], ALU.mult)
            bias = keep.tile([P, PACK], F32, name=name)
            nc.gpsimd.tensor_scalar(bias[:], product[:], -1.0, 0.0, ALU.mult, ALU.add)
            return bias

        warm_in = keep.tile([P, 1], F32, name="warm_in")
        warm_out = keep.tile([P, 1], F32, name="warm_out")
        nc.vector.memset(warm_in[:], 0.0)
        nc.scalar.activation(warm_out[:], warm_in[:], ACT.Sigmoid)

        scale_table = keep.tile([P, T], U8, name="scale_table")
        nc.gpsimd.memset(scale_table[:].bitcast(I32), 0)
        w_rows = w1.rearrange("(p j) c -> p j c", j=PACK)
        w_raw = [keep.tile([P, PACK, HALF], F32, name="w_raw%d" % h) for h in range(2)]
        nc.sync.dma_start(out=w_raw[0][:], in_=w_rows[:, :, :HALF])
        offs_sb = load_list("offs_sb", offs)
        for q in range(4):
            nc.sync.dma_start(
                out=scale_table[32 * q : 32 * q + 4, :].bitcast(I32),
                in_=x_scales[0, 4 * q : 4 * q + 4, :].bitcast(I32),
            )
        nc.sync.dma_start(out=w_raw[1][:], in_=w_rows[:, :, HALF:])
        word_table = keep.tile([P, T], U32, name="word_table")
        nc.sync.dma_start(
            out=word_table[:].bitcast(I32),
            in_=x_words[0].rearrange("p n r -> p (n r)").bitcast(I32),
        )
        sl2_sb = load_by_feature("sl2_sb", sl2)
        th2_sb = load_by_feature("th2_sb", th2)
        n2_sb = load_list("n2_sb", n2)
        n3_sb = load_list("n3_sb", n3)
        n1_sb = load_list("n1_sb", n1)
        sl_sb = load_by_feature("sl_sb", sl)
        th_sb = load_by_feature("th_sb", th)
        gb_sb = load_by_feature("gb_sb", gb)
        ga_sb = load_by_feature("ga_sb", ga)
        tau_sb = keep.tile([P, BLOCKS], F32, name="tau_sb")
        with nc.allow_non_contiguous_dma(reason="row 128 b + p of s lies on partition p of block b"):
            nc.sync.dma_start(out=tau_sb[:], in_=tau.rearrange("(b p) o -> p (b o)", p=P))
        n4_sb = load_list("n4_sb", n4)
        n5_sb = load_list("n5_sb", n5)
        bias2 = sigmoid_bias("bias2", sl2_sb, th2_sb)
        ident = keep.tile([P, P], F32, name="ident")
        make_identity(nc, ident[:])
        bias1 = sigmoid_bias("bias1", sl_sb, th_sb)
        neg_tau = keep.tile([P, BLOCKS], F32, name="neg_tau")
        nc.gpsimd.tensor_scalar(neg_tau[:], tau_sb[:], -1.0, 0.0, ALU.mult, ALU.add)
        ga_by_column = ga_sb[:].unsqueeze(1).to_broadcast([P, P, PACK])

        y_win = [keep.tile([P, WINDOW], F32, name="y_win%d" % t) for t in range(PACK)]
        s_win = [keep.tile([P, WINDOW], F32, name="s_win%d" % b) for b in range(BLOCKS)]
        sg2 = [win[:, S:] for win in s_win]
        for win in y_win:
            nc.vector.memset(win[:, S:], 0.0)

        w_grouped = scratch("w_grouped", [P, PACK, P, PACK], BF16)
        for h, cast in enumerate((nc.scalar.copy, nc.vector.tensor_copy)):
            cast(
                w_grouped[:, :, h * (P // 2) : (h + 1) * (P // 2), :],
                w_raw[h][:].rearrange("p j (m t) -> p t m j", t=PACK),
            )
        x_scale = scratch("x_scale", [P, S], U8)
        nc.vector.tensor_copy(x_scale[:], scale_table[:].indirect(offs_sb[:]))
        w_codes = scratch("w_codes", [P, S], U32)
        w_scale = scratch("w_scale", [P, S], U8)
        nc.vector.quantize_mx(
            out=w_codes[:].bitcast(FP8X4),
            scales=w_scale[:],
            in_=w_grouped[:].rearrange("p t m j -> p (t m j)"),
        )
        x_codes = scratch("x_codes", [P, S], U32)
        for first in (0, HALF):
            nc.vector.tensor_copy(
                x_codes[:, first : first + HALF],
                word_table[:].indirect(entries(offs_sb, first, first + HALF)),
            )

        def product_bank(name, shape):
            return psum.tile(shape, F32, name=name, tag="product", bufs=PRODUCT_BANKS)

        def turning_bank(name, shape):
            return psum.tile(shape, F32, name=name, tag="turning")

        def first_product(t, first, stop, bank, copy):
            features = slice(t * P, (t + 1) * P)
            acc = bank("y_acc%d_%d" % (t, first), [P, stop - first])
            nc.tensor.matmul_mx(
                out=acc[:],
                lhsT=w_codes[:, features].bitcast(FP8X4),
                lhsT_scale=w_scale[:, features],
                rhs=x_codes[:, first:stop].bitcast(FP8X4),
                rhs_scale=x_scale[:, first:stop],
                start=True,
                stop=True,
            )
            copy(y_win[t][:, first:stop], acc[:])

        first_product(0, 0, HALF, turning_bank, nc.scalar.copy)
        first_product(0, HALF, S, product_bank, nc.scalar.copy)
        for t in range(1, PACK):
            first_product(t, 0, S, product_bank, nc.vector.tensor_copy)

        for t in range(PACK):
            nc.scalar.activation(
                sg2[t], y_win[t][:].indirect(n2_sb[:]), ACT.Sigmoid,
                bias=bias2[:, t : t + 1], scale=sl2_sb[:, t : t + 1],
            )
        sg = {}
        for b in range(BLOCKS):
            for t in range(PACK):
                tile = scratch("sg%d_%d" % (b, t), [P, S], F32)
                nc.scalar.activation(
                    tile[:], y_win[t][:].indirect(entries(n1_sb, b * S, (b + 1) * S)), ACT.Sigmoid,
                    bias=bias1[:, t : t + 1], scale=sl_sb[:, t : t + 1],
                )
                sg[b, t] = tile[:].rearrange("p (j u) -> p j u", u=MEMBERS)

        y3, gated, larger2 = {}, {}, {}
        z2_rows = scratch("z2_rows", [P, PACK, S], BF16)
        z2_grouped = scratch("z2_grouped", [P, S, PACK], BF16)
        z2_codes = scratch("z2_codes", [P, S], U32)
        z2_scale = scratch("z2_scale", [P, S], U8)

        def apply_gate(t, after=None):
            gated[t] = scratch("gated%d" % t, [P, S], F32, after)
            nc.gpsimd.tensor_tensor(gated[t][:], y_win[t][:, :S], sg2[t], ALU.mult)

        def fetch3(t):
            y3[t] = scratch("y3_%d" % t, [P, S], F32)
            nc.vector.tensor_copy(y3[t][:], y_win[t][:].indirect(n3_sb[:]))

        def compare2(t):
            larger2[t] = scratch("larger2_%d" % t, [P, S], F32)
            nc.vector.scalar_tensor_tensor(larger2[t][:], y3[t][:], 0.75, gated[t][:], ALU.mult, ALU.max)

        def weigh2(t, engine):
            engine.tensor_scalar(z2_rows[:, t, :], larger2[t][:], gb_sb[:, t : t + 1], 0.0, ALU.mult, ALU.add)

        def group2():
            nc.vector.tensor_copy(
                out=z2_grouped[:].rearrange("p (c i) t -> p c t i", i=4),
                in_=z2_rows[:].rearrange("p t (c i) -> p c t i", i=4),
            )

        def quantise2():
            nc.vector.quantize_mx(
                out=z2_codes[:].bitcast(FP8X4), scales=z2_scale[:],
                in_=z2_grouped[:].rearrange("p c t -> p (c t)"),
            )

        y_turned, cnt, larger, back, z_grouped, z_codes, z_scale, s_acc, exp_bias = ({} for name in range(9))

        def turn_y(b):
            turn = product_bank("y_turn%d" % b, [P, PACK, P])
            for t in range(PACK):
                nc.tensor.transpose(turn[:, t, :], y_win[t][:, b * P : (b + 1) * P], ident[:])
            y_turned[b] = scratch("y_turned%d" % b, [P, S], F32)
            nc.vector.tensor_copy(y_turned[b][:], turn[:].rearrange("j t p -> j (t p)"))

        def pair_tile(name, n, after):
            tile = scratch(name, [P, n * 2 * P], F32, after)
            return tile[:].rearrange("p (j u) -> p j u", u=2)

        def add_pairs(engine, pairs, b, t):
            engine.tensor_tensor(pairs, sg[b, t][:, :, 0:2], sg[b, t][:, :, 2:4], ALU.add)

        def count(b, t, pairs=None):
            if t == 0:
                cnt[b] = psum.tile([P, PACK, P], F32, name="cnt%d" % b, tag="cnt", bufs=COUNT_BANKS)
            terms = sg[b, t]
            if pairs is not None:
                add_pairs(nc.vector, pairs, b, t)
                terms = pairs
            n = terms.shape[2]
            for u in range(n):
                nc.tensor.matmul(
                    cnt[b][:, t, :], terms[:, :, u], ident[:],
                    start=(u == 0), stop=(u == n - 1), is_transpose=True,
                )

        def compare(b, after=None):
            larger[b] = scratch("larger%d" % b, [P, PACK, P], F32, after)
            nc.vector.scalar_tensor_tensor(
                larger[b][:].rearrange("j t p -> j (t p)"), cnt[b][:].rearrange("j t p -> j (t p)"), -1.5,
                y_turned[b][:], ALU.add, ALU.max,
            )
            back[b] = turning_bank("back%d" % b, [P, PACK, P])
            for t in range(PACK):
                nc.tensor.transpose(back[b][:, t, :], larger[b][:, t, :], ident[:])

        def weigh(b, after=None):
            z_grouped[b] = scratch("z_grouped%d" % b, [P, P, PACK], BF16, after)
            nc.vector.tensor_tensor(z_grouped[b][:], back[b][:].rearrange("p t j -> p j t"), ga_by_column, ALU.mult)

        def second_product(b):
            z_codes[b] = scratch("z_codes%d" % b, [P, P], U32)
            z_scale[b] = scratch("z_scale%d" % b, [P, P], U8)
            nc.vector.quantize_mx(
                out=z_codes[b][:].bitcast(FP8X4), scales=z_scale[b][:],
                in_=z_grouped[b][:].rearrange("p j t -> p (j t)"),
            )
            s_acc[b] = product_bank("s_acc%d" % b, [P, S])
            nc.tensor.matmul_mx(
                out=s_acc[b][:],
                lhsT=z_codes[b][:].bitcast(FP8X4),
                lhsT_scale=z_scale[b][:],
                rhs=z2_codes[:].bitcast(FP8X4),
                rhs_scale=z2_scale[:],
                start=True,
                stop=True,
            )

        def leave_bank(b, engine):
            low = scratch("low%d" % b, [P, 1], F32)
            nc.vector.tensor_scalar(s_win[b][:, :S], s_acc[b][:], 0.0625, None, ALU.mult, ALU.min, accum_out=low[:])
            exp_bias[b] = keep.tile([P, 1], F32, name="exp_bias%d" % b)
            engine.tensor_tensor(exp_bias[b][:], low[:], tau_sb[:, b : b + 1], ALU.mult)

        s5 = {}

        def fetch5_on_vector(b, after):
            s5[b] = scratch("s5_%d" % b, [P, S], F32, after)
            nc.vector.tensor_copy(s5[b][:], s_win[b][:].indirect(n5_sb[:]))

        def fetch5_on_scalar(b):
            s5[b] = scratch("s5_%d" % b, [P, S], F32)
            nc.scalar.activation(s5[b][:], s_win[b][:].indirect(n5_sb[:]), ACT.Copy)

        for t in (0, 1):
            apply_gate(t)
        for t in (0, 1):
            fetch3(t)
        turn_y(0)
        for t in (0, 1):
            compare2(t)
        apply_gate(2, after="y3_1")
        apply_gate(3, after="gated0")
        weigh2(0, nc.gpsimd)
        for t in (2, 3):
            fetch3(t)
        for b in (1, 2):
            turn_y(b)
        for t in range(PACK):
            count(0, t)
        for t in (0, 1):
            count(1, t)
        for t in (2, 3):
            compare2(t)
        for t in (1, 2):
            weigh2(t, nc.vector)
        compare(0, after="y3_2")
        weigh2(3, nc.vector)
        group2()

        pairs = pair_tile("pairs1_late", 2, after="z2_rows")
        for k, t in enumerate((2, 3)):
            count(1, t, pairs[:, k * P : (k + 1) * P, :])
        weigh(0, after="larger2_3")
        quantise2()
        second_product(0)
        compare(1)
        leave_bank(0, nc.gpsimd)
        pairs = pair_tile("pairs2_early", 2, after="y_turned1")
        count(2, 0, pairs[:, :P, :])
        weigh(1)
        count(2, 1, pairs[:, P:, :])
        second_product(1)
        pairs = pair_tile("pairs2_late", 2, after="z_grouped1")
        for k, t in enumerate((2, 3)):
            count(2, t, pairs[:, k * P : (k + 1) * P, :])
        leave_bank(1, nc.gpsimd)
        last_pairs = pair_tile("last_pairs", LAST_TILE, after="z_codes1")
        for t in range(LAST_TILE):
            add_pairs(nc.gpsimd, last_pairs[:, t * P : (t + 1) * P, :], LAST, t)
        compare(2)
        fetch5_on_vector(0, after="y_turned2")
        weigh(2)

        last_columns = slice(LAST * P, S)
        back[LAST] = keep.tile([P, PACK, P], F32, name="last_larger")
        last_cnt = scratch("last_cnt", [P, LAST_TILE * P], F32, after="larger2")
        nc.vector.scalar_tensor_tensor(last_cnt[:], last_pairs[:, :, 0], -1.5, last_pairs[:, :, 1], ALU.add, ALU.add)
        second_product(2)
        for t in range(LAST_TILE):
            nc.vector.tensor_tensor(
                back[LAST][:, t, :], last_cnt[:, t * P : (t + 1) * P], y_win[t][:, last_columns], ALU.max
            )
        final_cnt = scratch("final_cnt", [P, P], F32, after="z_grouped2")
        nc.vector.tensor_reduce(final_cnt[:], sg[LAST, LAST_TILE], mybir.AxisListType.X, ALU.add)
        nc.vector.scalar_tensor_tensor(
            back[LAST][:, LAST_TILE, :], final_cnt[:], -1.5, y_win[LAST_TILE][:, last_columns], ALU.add, ALU.max
        )
        leave_bank(2, nc.vector)
        weigh(LAST)
        second_product(LAST)

        ea = keep.tile([P, BLOCKS, S], F32, name="ea")
        weighted = scratch("weighted", [P, BLOCKS, S], F32, after="z_grouped%d" % LAST)

        def decay(b, first=0, stop=S):
            nc.scalar.activation(
                ea[:, b, first:stop], s_win[b][:].indirect(entries(n4_sb, first, stop)), ACT.Exp,
                bias=exp_bias[b][:], scale=neg_tau[:, b : b + 1],
            )

        def weight5(b, first=0, stop=S):
            looked_up = s5[b][:, first:stop] if b in s5 else s_win[b][:].indirect(n5_sb[:])
            nc.vector.tensor_tensor(weighted[:, b, first:stop], looked_up, ea[:, b, first:stop], ALU.mult)

        def finish(b, first=0, stop=S):
            result = keep.tile([P, stop - first], F32, name="result%d_%d" % (b, first))
            nc.vector.scalar_tensor_tensor(
                result[:], weighted[:, b, first:stop], -2.0, s_win[b][:, first:stop], ALU.mult, ALU.add
            )
            nc.sync.dma_start(out=out[b * P : (b + 1) * P, first:stop], in_=result[:])

        for b in range(LAST):
            decay(b)
        fetch5_on_scalar(2)
        weight5(0)
        leave_bank(LAST, nc.vector)
        fetch5_on_scalar(LAST)
        for first in (0, HALF):
            decay(LAST, first, first + HALF)
        finish(0)
        for b in (1, 2):
            weight5(b)
        for b in (1, 2):
            finish(b)
        for first in (0, HALF):
            weight5(LAST, first, first + HALF)
        for first in (0, HALF):
            finish(LAST, first, first + HALF)
